import numpy as np
import ml_dtypes


def mxq(x, axis, fmt="e4m3"):
    dtype, down = {"e4m3": (ml_dtypes.float8_e4m3fn, 7), "e5m2": (ml_dtypes.float8_e5m2, 14)}[fmt]
    v = np.moveaxis(np.asarray(x, np.float32).astype(ml_dtypes.bfloat16).astype(np.float64), axis, -1)
    blocks = v.reshape(v.shape[:-1] + (-1, 32))
    amax = np.abs(blocks).max(-1, keepdims=True)
    byte = np.maximum(np.where(amax > 0, np.frexp(amax)[1] - 1 + 127, 0) - down, 1)
    scale = np.exp2(byte - 127.0)
    codes = (blocks / scale).astype(np.float32).astype(dtype).astype(np.float64)
    return np.moveaxis((codes * scale).reshape(v.shape), -1, axis)


WIDE = False


def mx_kscale(k):
    if not WIDE:
        return np.ones(k)
    levels = np.array([10, -10, 5, -5, 0])
    if k % 512:
        return np.exp2(np.random.permutation(np.resize(levels, k // 32))).repeat(32)
    a = np.empty((k // 512, 16))
    for p in range(k // 512):
        a[p, :8] = np.random.permutation(np.resize(levels, 8))
        for g in range(8):
            far = levels[np.abs(levels - a[p, g]) >= 10]
            a[p, g + 8] = far[np.random.randint(len(far))]
    return np.exp2(a.ravel()).repeat(32)


def f64(x):
    return np.asarray(x).astype(np.float64)


def striped(idx):
    return np.tile(idx.reshape(-1, 16).T, (8, 1)).astype(np.uint16)


def unstriped(offs):
    return offs[:16].T.reshape(-1).astype(np.int64)


def striped8(idx):
    return np.concatenate([x.reshape(-1, 16).T for x in idx]).astype(np.uint16)


def runs(offs, k):
    lists = np.stack([offs[16 * r : 16 * r + 16].T.reshape(-1) for r in range(8)]).astype(np.int64)
    return lists[np.arange(k) % 512 // 64]


def pack_weight(w):
    k, n = w.shape
    w = f64(np.asarray(w, np.float32).astype(ml_dtypes.bfloat16)).reshape(k // 32, 32, n)
    amax = np.abs(w).max(1)
    byte = np.clip(np.where(amax > 0, np.frexp(amax)[1] - 1 + 127 - 7, 1), 1, 254)
    scaled = (w * np.exp2(127.0 - byte)[:, None, :]).reshape(k, n).astype(np.float32)
    words = np.ascontiguousarray(scaled.reshape(k // 512, 128, 4, n).transpose(0, 1, 3, 2)).astype(ml_dtypes.float8_e4m3fn).view(np.uint8)
    return words, np.ascontiguousarray(byte.astype(np.uint8).reshape(k // 512, 16, n))


def unpack_weight(words, scales):
    g, p, n, _ = words.shape
    vals = np.ascontiguousarray(words).view(ml_dtypes.float8_e4m3fn).astype(np.float64) * np.repeat(np.exp2(scales.astype(np.float64) - 127.0), 8, axis=1)[..., None]
    return vals.transpose(0, 1, 3, 2).reshape(g * 512, n)


def sigmoid(v):
    return 1.0 / (1.0 + np.exp(-np.maximum(v, -700.0)))


K, T, S, N, H, W, G = 512, 2048, 512, 512, 512, 256, 2048


def setup_inputs():
    n = np.random.standard_normal
    s = mx_kscale(K)[:, None]
    u = mx_kscale(S)
    packed_xT = pack_weight(n((K, T)) * s)
    packed_dT = pack_weight(n((K, G)) / s)
    perm = np.stack([np.random.permutation(S) for _ in range(8)])
    return {
        "x_words": packed_xT[0],
        "x_scales": packed_xT[1],
        "w1": (n((K, H)) / np.sqrt(K) / s).astype(np.float32),
        "gn": (np.random.uniform(0.5, 1.5, (H, 1)) * u[:, None]).astype(np.float32),
        "w2": (n((H, N)) / np.sqrt(H) / u[:, None]).astype(np.float32),
        "d_words": packed_dT[0],
        "d_scales": packed_dT[1],
        "offs": striped(np.random.permutation(T)[:S]),
        "n1": striped8(perm[:, :W]),
        "n2": striped8(perm[:, W:]),
        "two": striped(np.random.permutation(T)[:S]),
        "k1": striped8(np.random.randint(0, G, (8, H))),
        "n3": striped(np.random.permutation(S)),
        "n4": striped(np.random.permutation(S)),
    }


def reference(x_words, x_scales, w1, gn, w2, d_words, d_scales, offs, n1, n2, two, k1, n3, n4):
    xq = unpack_weight(x_words, x_scales)[:, unstriped(offs)]
    y = mxq(f64(w1), 0, "e4m3").T @ xq
    pa = y[np.arange(H)[:, None], runs(n1, H)]
    pb = y[np.arange(H)[:, None], runs(n2, H)]
    ra = pa * sigmoid(pb)
    ds = y.copy()
    ds[np.arange(H)[:, None], runs(n2, H)] = ra
    z = f64(gn) * ds
    a = mxq(f64(w2), 0, "e4m3").T @ mxq(z, 0, "e4m3")
    d_k1 = unpack_weight(d_words, d_scales)[np.arange(K)[:, None], runs(k1, K)]
    x_two = unpack_weight(x_words, x_scales)[:, unstriped(two)]
    b = 0.0625 * (d_k1.T @ x_two)
    return a + (sigmoid(b[:, unstriped(n4)] - b)) * (a[:, unstriped(n3)] - a)

@@ -1,0 +1,243 @@
+from contextlib import ExitStack
+
+import concourse.mybir as mybir
+from concourse.masks import make_identity
+
+F32 = mybir.dt.float32
+BF16 = mybir.dt.bfloat16
+U32 = mybir.dt.uint32
+I32 = mybir.dt.int32
+U16 = mybir.dt.uint16
+U8 = mybir.dt.uint8
+FP8X4 = mybir.dt.float8_e4m3fn_x4
+ACT = mybir.ActivationFunctionType
+ALU = mybir.AluOpType
+
+P = 128
+PACK = 4
+TABLE = 2048
+S = 512
+HALF = S // 2
+TILES = S // P
+
+FLOPS = 3 * 2 * 512 * 512 * 512
+
+
+def tile_picked_cdjoinpullbfold_none_p_kernel(
+    tc, x_words, x_scales, w1, gn, w2, d_words, d_scales, offs, n1, n2, two, k1, n3, n4, out
+):
+    nc = tc.nc
+    with ExitStack() as ctx:
+        keep = ctx.enter_context(tc.tile_pool(name="keep", bufs=1))
+        ring = ctx.enter_context(tc.tile_pool(name="ring", bufs=2))
+        psum = ctx.enter_context(tc.psum_pool(name="psum", bufs=1))
+
+        def load_list(name, source):
+            lst = keep.tile(list(source.shape), U16, name=name)
+            nc.sync.dma_start(lst[:], source)
+            return lst
+
+        def words_of(table):
+            return table[0].rearrange("p n t -> p (n t)").bitcast(I32)
+
+        def gather(name, dtype, window, lst, tag=""):
+            picked = keep.tile([P, S], dtype, name=name, tag=tag, align_bytes=64)
+            nc.vector.tensor_copy(picked[:], window[:].indirect(lst[:]))
+            return picked
+
+        def quantise(name, values):
+            codes = keep.tile([P, S], U32, name=name + "_codes", align_bytes=64)
+            scales = keep.tile([P, S], U8, name=name + "_scales", align_bytes=64)
+            nc.vector.quantize_mx(out=codes[:].bitcast(FP8X4), scales=scales[:], in_=values[:])
+            return codes, scales
+
+        def product(bank, left, cols, right):
+            nc.tensor.matmul_mx(
+                out=bank[:],
+                lhsT=left[0][:, cols].bitcast(FP8X4),
+                lhsT_scale=left[1][:, cols],
+                rhs=right[0][:].bitcast(FP8X4),
+                rhs_scale=right[1][:],
+                start=True,
+                stop=True,
+            )
+
+        def block(jb):
+            return slice(P * jb, P * (jb + 1))
+
+        def pull_negated(engine_copy, name, window, lst, picked):
+            for h in range(2):
+                engine_copy(picked[:, HALF * h : HALF * (h + 1)], window[:].indirect(lst[:, 16 * h : 16 * (h + 1)]))
+
+        def scalar_negate(dst, src):
+            nc.scalar.activation(dst, src, ACT.Copy, scale=-1.0)
+
+        def difference_transposed(bank, plain, negated):
+            for jb in range(TILES):
+                nc.tensor.matmul(bank[:, block(jb)], plain[:, block(jb)], ident[:], start=(jb == 0), stop=False, is_transpose=True)
+            for jb in range(TILES):
+                nc.tensor.matmul(bank[:, block(jb)], negated[:, block(jb)], ident[:], start=False, stop=(jb == TILES - 1), is_transpose=True)
+
+        x_scale_table = keep.tile([P, TABLE], U8)
+        d_scale_table = keep.tile([P, TABLE], U8)
+        nc.gpsimd.memset(x_scale_table[:].bitcast(I32), 0)
+        nc.vector.memset(d_scale_table[:].bitcast(I32), 0)
+
+        def load_half(name, weight, h):
+            rows = weight.rearrange("(p j) c -> p j c", j=PACK)
+            half = keep.tile([P, PACK, HALF], F32, name="%s_raw%d" % (name, h))
+            nc.sync.dma_start(half[:], rows[:, :, HALF * h : HALF * (h + 1)])
+            return half
+
+        offs_l = load_list("offs_l", offs)
+        k1_l = load_list("k1_l", k1)
+        nc.sync.dma_start(d_scale_table[0:P:8, :].bitcast(I32), d_scales[0].bitcast(I32))
+        for q in range(4):
+            nc.sync.dma_start(x_scale_table[32 * q : 32 * q + 4, :].bitcast(I32), x_scales[0, 4 * q : 4 * q + 4, :].bitcast(I32))
+        w1_raw = [load_half("w1", w1, 0)]
+        two_l = load_list("two_l", two)
+        w1_raw.append(load_half("w1", w1, 1))
+        n2_l = load_list("n2_l", n2)
+        n1_l = load_list("n1_l", n1)
+        x_word_table = keep.tile([P, TABLE], U32)
+        nc.sync.dma_start(x_word_table[:].bitcast(I32), words_of(x_words))
+        w2_raw = [load_half("w2", w2, 0)]
+        d_word_table = keep.tile([P, TABLE], U32)
+        nc.sync.dma_start(d_word_table[:].bitcast(I32), words_of(d_words))
+        w2_raw.append(load_half("w2", w2, 1))
+        ident = keep.tile([P, P], F32)
+        make_identity(nc, ident[:])
+        gain = keep.tile([P, PACK], F32)
+        nc.gpsimd.dma_start(gain[:], gn.rearrange("(p t) o -> p (t o)", t=PACK))
+
+        w1_woven = keep.tile([P, PACK * S], BF16, align_bytes=64)
+        w1_view = w1_woven[:].rearrange("p (t m j) -> p m j t", t=PACK, j=PACK)
+        w1_halves = [raw[:].rearrange("p j (m t) -> p m j t", t=PACK) for raw in w1_raw]
+        nc.scalar.copy(w1_view[:, :64], w1_halves[0])
+        nc.scalar.copy(w1_view[:, 64 : 64 + 32], w1_halves[1][:, :32])
+        dk_scales = gather("dk_scales", U8, d_scale_table, k1_l)
+        xo_scales = gather("xo_scales", U8, x_scale_table, offs_l)
+        xt_scales = gather("xt_scales", U8, x_scale_table, two_l)
+        nc.vector.tensor_copy(w1_view[:, 64 + 32 :], w1_halves[1][:, 32:])
+        w1_q = []
+        for t in range(TILES):
+            codes = keep.tile([P, P], U32, name="w1_codes%d" % t, align_bytes=64)
+            scales = keep.tile([P, P], U8, name="w1_scales%d" % t, align_bytes=64)
+            nc.vector.quantize_mx(out=codes[:].bitcast(FP8X4), scales=scales[:], in_=w1_woven[:, S * t : S * (t + 1)])
+            w1_q.append((codes, scales))
+        xo_words = gather("xo_words", U32, x_word_table, offs_l)
+        y_banks = []
+        for t in range(TILES):
+            y_bank = psum.tile([P, S], F32, name="y_bank", tag="bank%d" % (0,1,2,3)[t])
+            product(y_bank, w1_q[t], block(0), (xo_words, xo_scales))
+            y_banks.append(y_bank)
+        xt_words = gather("xt_words", U32, x_word_table, two_l)
+        d_scale_plane = keep.tile([P, S], U8, tag="w1_codes0", align_bytes=64)
+        nc.vector.memset(d_scale_plane[:].bitcast(I32), 0)
+        for r in range(4):
+            queue = nc.scalar if r < 4 else nc.sync
+            queue.dma_start(d_scale_plane[r:P:32, :].bitcast(I32), dk_scales[8 * r : P : 32, :].bitcast(I32))
+        n4_l = load_list("n4_l", n4)
+        n3_l = load_list("n3_l", n3)
+        dk_words = gather("dk_words", U32, d_word_table, k1_l)
+
+        w2_codes = keep.tile([P, S], U32, align_bytes=64)
+        w2_scales = keep.tile([P, S], U8, align_bytes=64)
+        for h, weave in enumerate((nc.vector.tensor_copy, nc.vector.tensor_copy)):
+            woven = keep.tile([P, PACK * HALF], BF16, name="w2_woven%d" % h, align_bytes=64)
+            weave(woven[:].rearrange("p (c i j) -> p c j i", i=4, j=PACK), w2_raw[h][:].rearrange("p j (c i) -> p c j i", i=4))
+            cols = slice(HALF * h, HALF * (h + 1))
+            nc.vector.quantize_mx(out=w2_codes[:, cols].bitcast(FP8X4), scales=w2_scales[:, cols], in_=woven[:])
+        w2_q = (w2_codes, w2_scales)
+
+        ys = []
+        for t in range(TILES):
+            y = keep.tile([P, S], F32, name="y%d" % t)
+            nc.scalar.copy(y[:], y_banks[t][:])
+            gate = keep.tile([P, HALF], F32, name="gate%d" % t)
+            nc.scalar.activation(gate[:], y[:].indirect(n2_l[:]), ACT.Sigmoid)
+            pa = keep.tile([P, HALF], F32, name="pa%d" % t)
+            nc.scalar.activation(pa[:], y[:].indirect(n1_l[:]), ACT.Copy)
+            nc.vector.tensor_tensor(y[:].indirect(n2_l[:]), pa[:], gate[:], ALU.mult)
+            ys.append(y)
+        z_rows = keep.tile([P, PACK, S], BF16, tag="pa3")
+        for t in range(TILES):
+            nc.vector.tensor_scalar(z_rows[:, t, :], ys[t][:], gain[:, t : t + 1], None, ALU.mult)
+        z_wovens = []
+        for h in range(2):
+            woven = keep.tile([P, PACK * HALF], BF16, name="z_woven%d" % h, align_bytes=64)
+            nc.vector.tensor_copy(
+                woven[:].rearrange("p (c i j) -> p c j i", i=4, j=PACK),
+                z_rows[:, :, HALF * h : HALF * (h + 1)].rearrange("p j (c i) -> p c j i", i=4),
+            )
+            z_wovens.append(woven)
+        z_q = []
+        for h in range(2):
+            codes = keep.tile([P, HALF], U32, name="z_codes%d" % h, align_bytes=64)
+            scales = keep.tile([P, HALF], U8, name="z_scales%d" % h, align_bytes=64)
+            nc.vector.quantize_mx(out=codes[:].bitcast(FP8X4), scales=scales[:], in_=z_wovens[h][:])
+            z_q.append((codes, scales))
+
+        b_banks = []
+        for t in range(TILES):
+            b_bank = psum.tile([P, S], F32, name="b_bank", tag="bank%d" % (4 + t))
+            product(b_bank, (dk_words, d_scale_plane), block(t), (xt_words, xt_scales))
+            b_banks.append(b_bank)
+
+        def blend_turned(t):
+            b = keep.tile([P, S], F32, name="b%d" % t)
+            nc.scalar.activation(b[:], b_banks[t][:], ACT.Copy, scale=0.0625)
+            b4 = keep.tile([P, S], F32, name="b4_%d" % t)
+            pull_negated(scalar_negate, "b4", b, n4_l, b4)
+            d_bank = psum.tile([P, S], F32, name="d_bank", tag="bank%d" % t)
+            difference_transposed(d_bank, b, b4)
+            blend = keep.tile([P, S], F32, name="blend%d" % t)
+            nc.scalar.activation(blend[:], d_bank[:], ACT.Sigmoid, scale=-1.0)
+            return blend
+
+        def turn_back(t, turned):
+            back_bank = psum.tile([P, S], F32, name="back_bank", tag="bank%d" % (4 + t))
+            for jb in range(TILES):
+                nc.tensor.transpose(back_bank[:, block(jb)], turned[:, block(jb)], ident[:])
+            return back_bank
+
+        ROUTE = "HHHH"
+        COPY = "VVSS"
+        PULL = "VSSS"
+        blends = [blend_turned(t) for t in range(3)]
+        rows = []
+        for t in range(TILES):
+            a_bank = psum.tile([P, S], F32, name="a_bank", tag="bank%d" % (t % 2))
+            for h in range(2):
+                product(a_bank[:, HALF * h : HALF * (h + 1)], w2_q, block(t), z_q[h])
+            a = keep.tile([P, S], F32, name="a%d" % t)
+            (nc.vector.tensor_copy if COPY[t] == "V" else nc.scalar.copy)(a[:], a_bank[:])
+            rows.append(a)
+        backs = [turn_back(t, blends[t]) for t in range(2)]
+        blends.extend(blend_turned(t) for t in range(3, TILES))
+        for t in range(TILES):
+            a = rows[t]
+            a3 = keep.tile([P, S], F32, name="a3_%d" % t)
+            res = keep.tile([P, S], F32, name="res%d" % t)
+            pull = keep.tile([P, S], F32, name="pull%d" % t)
+            if ROUTE[t] == "P":
+                pull_negated(scalar_negate, "a3", a, n3_l, a3)
+                e_bank = psum.tile([P, S], F32, name="e_bank", tag="bank%d" % (2 + t % 2))
+                difference_transposed(e_bank, a, a3)
+                nc.vector.tensor_tensor(pull[:], e_bank[:], blends[t][:], ALU.mult)
+                back_bank = turn_back(t, pull)
+                nc.vector.tensor_tensor(res[:], a[:], back_bank[:], ALU.subtract)
+                nc.sync.dma_start(out[block(t), :], res[:])
+            else:
+                back_bank = backs[t] if t < len(backs) else turn_back(t, blends[t])
+                if PULL[t] == "V":
+                    pull_negated(nc.vector.tensor_copy, "a3", a, n3_l, a3)
+                else:
+                    pull_negated(lambda dst, src: nc.scalar.activation(dst, src, ACT.Copy), "a3", a, n3_l, a3)
+                step = keep.tile([P, S], F32, name="step%d" % t)
+                parts = [slice(0, HALF), slice(HALF, S)] if ROUTE[t] == "H" else [slice(0, S)]
+                for c in parts:
+                    nc.vector.tensor_tensor(step[:, c], a3[:, c], a[:, c], ALU.subtract)
+                    nc.vector.tensor_tensor(pull[:, c], back_bank[:, c], step[:, c], ALU.mult)
+                    nc.vector.tensor_tensor(res[:, c], pull[:, c], a[:, c], ALU.add)
+                    nc.sync.dma_start(out[block(t), c], res[:, c])

@@ -82,6 +82,10 @@ def tile_picked_cdjoinpullbfold_none_p_kernel(
         d_scale_table = keep.tile([P, TABLE], U8)
         nc.gpsimd.memset(x_scale_table[:].bitcast(I32), 0)
         nc.vector.memset(d_scale_table[:].bitcast(I32), 0)
+        warm = keep.tile([P, 1], F32)
+        nc.vector.memset(warm[:], 0.0)
+        warmed = keep.tile([P, 1], F32)
+        nc.scalar.activation(warmed[:], warm[:], ACT.Sigmoid)
 
         def load_half(name, weight, h):
             rows = weight.rearrange("(p j) c -> p j c", j=PACK)

@@ -80,8 +80,8 @@ def tile_picked_cdjoinpullbfold_none_p_kernel(
 
         x_scale_table = keep.tile([P, TABLE], U8)
         d_scale_table = keep.tile([P, TABLE], U8)
-        nc.gpsimd.memset(x_scale_table[:].bitcast(I32), 0)
-        nc.vector.memset(d_scale_table[:].bitcast(I32), 0)
+        nc.gpsimd.memset(d_scale_table[:].bitcast(I32), 0)
+        nc.vector.memset(x_scale_table[:].bitcast(I32), 0)
         warm = keep.tile([P, 1], F32)
         nc.vector.memset(warm[:], 0.0)
         warmed = keep.tile([P, 1], F32)
@@ -101,10 +101,10 @@ def tile_picked_cdjoinpullbfold_none_p_kernel(
         w1_raw = [load_half("w1", w1, 0)]
         two_l = load_list("two_l", two)
         w1_raw.append(load_half("w1", w1, 1))
-        n2_l = load_list("n2_l", n2)
-        n1_l = load_list("n1_l", n1)
         x_word_table = keep.tile([P, TABLE], U32)
         nc.sync.dma_start(x_word_table[:].bitcast(I32), words_of(x_words))
+        n2_l = load_list("n2_l", n2)
+        n1_l = load_list("n1_l", n1)
         w2_raw = [load_half("w2", w2, 0)]
         d_word_table = keep.tile([P, TABLE], U32)
         nc.sync.dma_start(d_word_table[:].bitcast(I32), words_of(d_words))
@@ -112,7 +112,7 @@ def tile_picked_cdjoinpullbfold_none_p_kernel(
         ident = keep.tile([P, P], F32)
         make_identity(nc, ident[:])
         gain = keep.tile([P, PACK], F32)
-        nc.gpsimd.dma_start(gain[:], gn.rearrange("(p t) o -> p (t o)", t=PACK))
+        nc.sync.dma_start(gain[:], gn.rearrange("(p t) o -> p (t o)", t=PACK))
 
         w1_woven = keep.tile([P, PACK * S], BF16, align_bytes=64)
         w1_view = w1_woven[:].rearrange("p (t m j) -> p m j t", t=PACK, j=PACK)
@@ -129,14 +129,17 @@ def tile_picked_cdjoinpullbfold_none_p_kernel(
             scales = keep.tile([P, P], U8, name="w1_scales%d" % t, align_bytes=64)
             nc.vector.quantize_mx(out=codes[:].bitcast(FP8X4), scales=scales[:], in_=w1_woven[:, S * t : S * (t + 1)])
             w1_q.append((codes, scales))
-        xo_words = gather("xo_words", U32, x_word_table, offs_l)
+        xo_words = keep.tile([P, S], U32, align_bytes=64)
+        for h in range(2):
+            nc.vector.tensor_copy(xo_words[:, HALF * h : HALF * (h + 1)], x_word_table[:].indirect(offs_l[:, 16 * h : 16 * (h + 1)]))
         y_banks = []
         for t in range(TILES):
             y_bank = psum.tile([P, S], F32, name="y_bank", tag="bank%d" % (0,1,2,3)[t])
-            product(y_bank, w1_q[t], block(0), (xo_words, xo_scales))
+            for c in (slice(0, HALF), slice(HALF, S)) if t == 0 else (slice(0, S),):
+                product(y_bank[:, c], w1_q[t], block(0), (xo_words[:, c], xo_scales[:, c]))
             y_banks.append(y_bank)
         xt_words = gather("xt_words", U32, x_word_table, two_l)
-        d_scale_plane = keep.tile([P, S], U8, tag="w1_codes0", align_bytes=64)
+        d_scale_plane = keep.tile([P, S], U8, tag="w1_codes1", align_bytes=64)
         nc.vector.memset(d_scale_plane[:].bitcast(I32), 0)
         for r in range(4):
             queue = nc.scalar if r < 4 else nc.sync
@@ -147,11 +150,16 @@ def tile_picked_cdjoinpullbfold_none_p_kernel(
 
         w2_codes = keep.tile([P, S], U32, align_bytes=64)
         w2_scales = keep.tile([P, S], U8, align_bytes=64)
-        for h, weave in enumerate((nc.vector.tensor_copy, nc.vector.tensor_copy)):
-            woven = keep.tile([P, PACK * HALF], BF16, name="w2_woven%d" % h, align_bytes=64)
-            weave(woven[:].rearrange("p (c i j) -> p c j i", i=4, j=PACK), w2_raw[h][:].rearrange("p j (c i) -> p c j i", i=4))
+
+        def quantise_w2(h, tag):
+            woven = keep.tile([P, PACK * HALF], BF16, name="w2_woven%d" % h, tag=tag, align_bytes=64)
+            nc.vector.tensor_copy(
+                woven[:].rearrange("p (c i j) -> p c j i", i=4, j=PACK), w2_raw[h][:].rearrange("p j (c i) -> p c j i", i=4)
+            )
             cols = slice(HALF * h, HALF * (h + 1))
             nc.vector.quantize_mx(out=w2_codes[:, cols].bitcast(FP8X4), scales=w2_scales[:, cols], in_=woven[:])
+
+        quantise_w2(0, "")
         w2_q = (w2_codes, w2_scales)
 
         ys = []
@@ -160,11 +168,11 @@ def tile_picked_cdjoinpullbfold_none_p_kernel(
             nc.scalar.copy(y[:], y_banks[t][:])
             gate = keep.tile([P, HALF], F32, name="gate%d" % t)
             nc.scalar.activation(gate[:], y[:].indirect(n2_l[:]), ACT.Sigmoid)
-            pa = keep.tile([P, HALF], F32, name="pa%d" % t)
+            pa = keep.tile([P, HALF], F32, name="pa%d" % t, align_bytes=64)
             nc.scalar.activation(pa[:], y[:].indirect(n1_l[:]), ACT.Copy)
             nc.vector.tensor_tensor(y[:].indirect(n2_l[:]), pa[:], gate[:], ALU.mult)
             ys.append(y)
-        z_rows = keep.tile([P, PACK, S], BF16, tag="pa3")
+        z_rows = keep.tile([P, PACK, S], BF16, tag="pa3", align_bytes=64)
         for t in range(TILES):
             nc.vector.tensor_scalar(z_rows[:, t, :], ys[t][:], gain[:, t : t + 1], None, ALU.mult)
         z_wovens = []
@@ -182,66 +190,89 @@ def tile_picked_cdjoinpullbfold_none_p_kernel(
             nc.vector.quantize_mx(out=codes[:].bitcast(FP8X4), scales=scales[:], in_=z_wovens[h][:])
             z_q.append((codes, scales))
 
+        quantise_w2(1, "pa3")
         b_banks = []
         for t in range(TILES):
             b_bank = psum.tile([P, S], F32, name="b_bank", tag="bank%d" % (4 + t))
             product(b_bank, (dk_words, d_scale_plane), block(t), (xt_words, xt_scales))
             b_banks.append(b_bank)
 
-        def blend_turned(t):
+        opened = {}
+
+        def blend_open(t):
             b = keep.tile([P, S], F32, name="b%d" % t)
             nc.scalar.activation(b[:], b_banks[t][:], ACT.Copy, scale=0.0625)
+            d_bank = psum.tile([P, S], F32, name="d_bank", tag="bank%d" % t)
+            for jb in range(TILES):
+                nc.tensor.matmul(d_bank[:, block(jb)], b[:, block(jb)], ident[:], start=(jb == 0), stop=False, is_transpose=True)
+            opened[t] = (b, d_bank)
+
+        def blend_close(t):
+            b, d_bank = opened[t]
             b4 = keep.tile([P, S], F32, name="b4_%d" % t)
             pull_negated(scalar_negate, "b4", b, n4_l, b4)
-            d_bank = psum.tile([P, S], F32, name="d_bank", tag="bank%d" % t)
-            difference_transposed(d_bank, b, b4)
+            for jb in range(TILES):
+                nc.tensor.matmul(d_bank[:, block(jb)], b4[:, block(jb)], ident[:], start=False, stop=(jb == TILES - 1), is_transpose=True)
             blend = keep.tile([P, S], F32, name="blend%d" % t)
             nc.scalar.activation(blend[:], d_bank[:], ACT.Sigmoid, scale=-1.0)
             return blend
 
         def turn_back(t, turned):
-            back_bank = psum.tile([P, S], F32, name="back_bank", tag="bank%d" % (4 + t))
+            back_bank = psum.tile([P, S], F32, name="back_bank", tag="bank%d" % t)
             for jb in range(TILES):
                 nc.tensor.transpose(back_bank[:, block(jb)], turned[:, block(jb)], ident[:])
             return back_bank
 
-        ROUTE = "HHHH"
         COPY = "VVSS"
-        PULL = "VSSS"
-        blends = [blend_turned(t) for t in range(3)]
-        rows = []
-        for t in range(TILES):
-            a_bank = psum.tile([P, S], F32, name="a_bank", tag="bank%d" % (t % 2))
+        blends = []
+        for t in range(2):
+            blend_open(t)
+            blends.append(blend_close(t))
+        blend_open(2)
+        a_banks, rows = {}, {}
+
+        def second_product(t):
+            a_banks[t] = psum.tile([P, S], F32, name="a_bank", tag="bank%d" % (4 + t))
             for h in range(2):
-                product(a_bank[:, HALF * h : HALF * (h + 1)], w2_q, block(t), z_q[h])
-            a = keep.tile([P, S], F32, name="a%d" % t)
-            (nc.vector.tensor_copy if COPY[t] == "V" else nc.scalar.copy)(a[:], a_bank[:])
-            rows.append(a)
-        backs = [turn_back(t, blends[t]) for t in range(2)]
-        blends.extend(blend_turned(t) for t in range(3, TILES))
-        for t in range(TILES):
-            a = rows[t]
+                product(a_banks[t][:, HALF * h : HALF * (h + 1)], w2_q, block(t), z_q[h])
+
+        def evacuate(t):
+            rows[t] = keep.tile([P, S], F32, name="a%d" % t)
+            (nc.vector.tensor_copy if COPY[t] == "V" else nc.scalar.copy)(rows[t][:], a_banks[t][:])
+
+        def pull_rows(t, engine_copy):
             a3 = keep.tile([P, S], F32, name="a3_%d" % t)
-            res = keep.tile([P, S], F32, name="res%d" % t)
+            pull_negated(engine_copy, "a3", rows[t], n3_l, a3)
+            return a3
+
+        def scalar_copy(dst, src):
+            nc.scalar.activation(dst, src, ACT.Copy)
+
+        def finish_plain(t, a3, blend_bank, tag, parts=(slice(0, HALF), slice(HALF, S))):
+            a = rows[t]
+            step = keep.tile([P, S], F32, name="step%d" % t, tag=tag)
             pull = keep.tile([P, S], F32, name="pull%d" % t)
-            if ROUTE[t] == "P":
-                pull_negated(scalar_negate, "a3", a, n3_l, a3)
-                e_bank = psum.tile([P, S], F32, name="e_bank", tag="bank%d" % (2 + t % 2))
-                difference_transposed(e_bank, a, a3)
-                nc.vector.tensor_tensor(pull[:], e_bank[:], blends[t][:], ALU.mult)
-                back_bank = turn_back(t, pull)
-                nc.vector.tensor_tensor(res[:], a[:], back_bank[:], ALU.subtract)
-                nc.sync.dma_start(out[block(t), :], res[:])
-            else:
-                back_bank = backs[t] if t < len(backs) else turn_back(t, blends[t])
-                if PULL[t] == "V":
-                    pull_negated(nc.vector.tensor_copy, "a3", a, n3_l, a3)
-                else:
-                    pull_negated(lambda dst, src: nc.scalar.activation(dst, src, ACT.Copy), "a3", a, n3_l, a3)
-                step = keep.tile([P, S], F32, name="step%d" % t)
-                parts = [slice(0, HALF), slice(HALF, S)] if ROUTE[t] == "H" else [slice(0, S)]
-                for c in parts:
-                    nc.vector.tensor_tensor(step[:, c], a3[:, c], a[:, c], ALU.subtract)
-                    nc.vector.tensor_tensor(pull[:, c], back_bank[:, c], step[:, c], ALU.mult)
-                    nc.vector.tensor_tensor(res[:, c], pull[:, c], a[:, c], ALU.add)
-                    nc.sync.dma_start(out[block(t), c], res[:, c])
+            res = keep.tile([P, S], F32, name="res%d" % t)
+            for c in parts:
+                nc.vector.tensor_tensor(step[:, c], a3[:, c], a[:, c], ALU.subtract)
+                nc.vector.tensor_tensor(pull[:, c], blend_bank[:, c], step[:, c], ALU.mult)
+                nc.vector.tensor_tensor(res[:, c], pull[:, c], a[:, c], ALU.add)
+                nc.sync.dma_start(out[block(t), c], res[:, c])
+
+        second_product(0)
+        second_product(1)
+        evacuate(0)
+        evacuate(1)
+        blends.append(blend_close(2))
+        backs = [turn_back(0, blends[0])]
+        blend_open(3)
+        second_product(2)
+        second_product(3)
+        backs.append(turn_back(1, blends[1]))
+        blends.append(blend_close(3))
+        finish_plain(0, pull_rows(0, nc.vector.tensor_copy), backs[0], "")
+        for t in range(1, TILES):
+            a3 = pull_rows(t, scalar_copy)
+            if t + 1 < TILES:
+                evacuate(t + 1)
+            finish_plain(t, a3, backs[t] if t < len(backs) else turn_back(t, blends[t]), "")

@@ -19,8 +19,12 @@ TABLE = 2048
 S = 512
 HALF = S // 2
 TILES = S // P
+HALVES = (slice(0, HALF), slice(HALF, S))
+LIST_HALVES = (slice(0, HALF // 16), slice(HALF // 16, S // 16))
+SPARE = 8
+RUN = 4
 
-FLOPS = 3 * 2 * 512 * 512 * 512
+FLOPS = 3 * 2 * S * S * S
 
 
 def tile_picked_cdjoinpullbfold_none_p_kernel(
@@ -29,140 +33,147 @@ def tile_picked_cdjoinpullbfold_none_p_kernel(
     nc = tc.nc
     with ExitStack() as ctx:
         keep = ctx.enter_context(tc.tile_pool(name="keep", bufs=1))
-        ring = ctx.enter_context(tc.tile_pool(name="ring", bufs=2))
         psum = ctx.enter_context(tc.psum_pool(name="psum", bufs=1))
 
+        def block(n):
+            return slice(P * n, P * (n + 1))
+
+        def bank(n, name):
+            return psum.tile([P, S], F32, name=name, tag="bank%d" % n)
+
         def load_list(name, source):
-            lst = keep.tile(list(source.shape), U16, name=name)
-            nc.sync.dma_start(lst[:], source)
-            return lst
+            offsets = keep.tile(list(source.shape), U16, name=name)
+            nc.sync.dma_start(offsets[:], source)
+            return offsets
 
-        def words_of(table):
-            return table[0].rearrange("p n t -> p (n t)").bitcast(I32)
+        def load_words(name, table):
+            words = keep.tile([P, TABLE], U32, name=name)
+            nc.sync.dma_start(words[:].bitcast(I32), table[0].rearrange("p n t -> p (n t)").bitcast(I32))
+            return words
 
-        def gather(name, dtype, window, lst, tag=""):
-            picked = keep.tile([P, S], dtype, name=name, tag=tag, align_bytes=64)
-            nc.vector.tensor_copy(picked[:], window[:].indirect(lst[:]))
+        def load_weight_half(name, weight, h):
+            half = keep.tile([P, PACK, HALF], F32, name="%s_raw%d" % (name, h))
+            nc.sync.dma_start(half[:], weight.rearrange("(p j) c -> p j c", j=PACK)[:, :, HALVES[h]])
+            return half
+
+        def gather_packed(name, dtype, table, offsets):
+            picked = keep.tile([P, S], dtype, name=name, align_bytes=64)
+            nc.vector.tensor_copy(picked[:], table[:].indirect(offsets[:]))
             return picked
 
-        def quantise(name, values):
-            codes = keep.tile([P, S], U32, name=name + "_codes", align_bytes=64)
-            scales = keep.tile([P, S], U8, name=name + "_scales", align_bytes=64)
-            nc.vector.quantize_mx(out=codes[:].bitcast(FP8X4), scales=scales[:], in_=values[:])
+        def gather_rows(name, copy, rows, offsets):
+            picked = keep.tile([P, S], F32, name=name)
+            for h in range(2):
+                copy(picked[:, HALVES[h]], rows[:].indirect(offsets[:, LIST_HALVES[h]]))
+            return picked
+
+        def scalar_copy(dst, src):
+            nc.scalar.activation(dst, src, ACT.Copy)
+
+        def weave(woven, rows):
+            nc.vector.tensor_copy(
+                woven.rearrange("p (c i j) -> p c j i", i=RUN, j=PACK), rows.rearrange("p j (c i) -> p c j i", i=RUN)
+            )
+
+        def quantise(name, width, values):
+            codes = keep.tile([P, width], U32, name=name + "_codes", align_bytes=64)
+            scales = keep.tile([P, width], U8, name=name + "_scales", align_bytes=64)
+            nc.vector.quantize_mx(out=codes[:].bitcast(FP8X4), scales=scales[:], in_=values)
             return codes, scales
 
-        def product(bank, left, cols, right):
+        def product(result, left, left_cols, right, right_cols):
             nc.tensor.matmul_mx(
-                out=bank[:],
-                lhsT=left[0][:, cols].bitcast(FP8X4),
-                lhsT_scale=left[1][:, cols],
-                rhs=right[0][:].bitcast(FP8X4),
-                rhs_scale=right[1][:],
+                out=result,
+                lhsT=left[0][:, left_cols].bitcast(FP8X4),
+                lhsT_scale=left[1][:, left_cols],
+                rhs=right[0][:, right_cols].bitcast(FP8X4),
+                rhs_scale=right[1][:, right_cols],
                 start=True,
                 stop=True,
             )
 
-        def block(jb):
-            return slice(P * jb, P * (jb + 1))
-
-        def pull_negated(engine_copy, name, window, lst, picked):
-            for h in range(2):
-                engine_copy(picked[:, HALF * h : HALF * (h + 1)], window[:].indirect(lst[:, 16 * h : 16 * (h + 1)]))
-
-        def scalar_negate(dst, src):
-            nc.scalar.activation(dst, src, ACT.Copy, scale=-1.0)
-
-        def difference_transposed(bank, plain, negated):
-            for jb in range(TILES):
-                nc.tensor.matmul(bank[:, block(jb)], plain[:, block(jb)], ident[:], start=(jb == 0), stop=False, is_transpose=True)
-            for jb in range(TILES):
-                nc.tensor.matmul(bank[:, block(jb)], negated[:, block(jb)], ident[:], start=False, stop=(jb == TILES - 1), is_transpose=True)
+        def add_turned(target, rows, opens):
+            for n in range(TILES):
+                nc.tensor.matmul(
+                    target[:, block(n)],
+                    rows[:, block(n)],
+                    ident[:],
+                    start=opens and n == 0,
+                    stop=not opens and n == TILES - 1,
+                    is_transpose=True,
+                )
 
         x_scale_table = keep.tile([P, TABLE], U8)
         d_scale_table = keep.tile([P, TABLE], U8)
         nc.gpsimd.memset(d_scale_table[:].bitcast(I32), 0)
         nc.vector.memset(x_scale_table[:].bitcast(I32), 0)
+
         warm = keep.tile([P, 1], F32)
         nc.vector.memset(warm[:], 0.0)
         warmed = keep.tile([P, 1], F32)
         nc.scalar.activation(warmed[:], warm[:], ACT.Sigmoid)
 
-        def load_half(name, weight, h):
-            rows = weight.rearrange("(p j) c -> p j c", j=PACK)
-            half = keep.tile([P, PACK, HALF], F32, name="%s_raw%d" % (name, h))
-            nc.sync.dma_start(half[:], rows[:, :, HALF * h : HALF * (h + 1)])
-            return half
-
         offs_l = load_list("offs_l", offs)
         k1_l = load_list("k1_l", k1)
         nc.sync.dma_start(d_scale_table[0:P:8, :].bitcast(I32), d_scales[0].bitcast(I32))
         for q in range(4):
-            nc.sync.dma_start(x_scale_table[32 * q : 32 * q + 4, :].bitcast(I32), x_scales[0, 4 * q : 4 * q + 4, :].bitcast(I32))
-        w1_raw = [load_half("w1", w1, 0)]
+            nc.sync.dma_start(
+                x_scale_table[32 * q : 32 * q + 4, :].bitcast(I32), x_scales[0, 4 * q : 4 * q + 4, :].bitcast(I32)
+            )
+        w1_raw = [load_weight_half("w1", w1, 0)]
         two_l = load_list("two_l", two)
-        w1_raw.append(load_half("w1", w1, 1))
-        x_word_table = keep.tile([P, TABLE], U32)
-        nc.sync.dma_start(x_word_table[:].bitcast(I32), words_of(x_words))
+        w1_raw.append(load_weight_half("w1", w1, 1))
+        x_word_table = load_words("x_word_table", x_words)
         n2_l = load_list("n2_l", n2)
         n1_l = load_list("n1_l", n1)
-        w2_raw = [load_half("w2", w2, 0)]
-        d_word_table = keep.tile([P, TABLE], U32)
-        nc.sync.dma_start(d_word_table[:].bitcast(I32), words_of(d_words))
-        w2_raw.append(load_half("w2", w2, 1))
+        w2_raw = [load_weight_half("w2", w2, 0)]
+        d_word_table = load_words("d_word_table", d_words)
+        w2_raw.append(load_weight_half("w2", w2, 1))
         ident = keep.tile([P, P], F32)
         make_identity(nc, ident[:])
         gain = keep.tile([P, PACK], F32)
         nc.sync.dma_start(gain[:], gn.rearrange("(p t) o -> p (t o)", t=PACK))
 
         w1_woven = keep.tile([P, PACK * S], BF16, align_bytes=64)
-        w1_view = w1_woven[:].rearrange("p (t m j) -> p m j t", t=PACK, j=PACK)
+        w1_dealt = w1_woven[:].rearrange("p (t m j) -> p m j t", t=PACK, j=PACK)
         w1_halves = [raw[:].rearrange("p j (m t) -> p m j t", t=PACK) for raw in w1_raw]
-        nc.scalar.copy(w1_view[:, :64], w1_halves[0])
-        nc.scalar.copy(w1_view[:, 64 : 64 + 32], w1_halves[1][:, :32])
-        dk_scales = gather("dk_scales", U8, d_scale_table, k1_l)
-        xo_scales = gather("xo_scales", U8, x_scale_table, offs_l)
-        xt_scales = gather("xt_scales", U8, x_scale_table, two_l)
-        nc.vector.tensor_copy(w1_view[:, 64 + 32 :], w1_halves[1][:, 32:])
-        w1_q = []
-        for t in range(TILES):
-            codes = keep.tile([P, P], U32, name="w1_codes%d" % t, align_bytes=64)
-            scales = keep.tile([P, P], U8, name="w1_scales%d" % t, align_bytes=64)
-            nc.vector.quantize_mx(out=codes[:].bitcast(FP8X4), scales=scales[:], in_=w1_woven[:, S * t : S * (t + 1)])
-            w1_q.append((codes, scales))
+        nc.scalar.copy(w1_dealt[:, : P // 2], w1_halves[0])
+        dk_scales = gather_packed("dk_scales", U8, d_scale_table, k1_l)
+        xo_scales = gather_packed("xo_scales", U8, x_scale_table, offs_l)
+        xt_scales = gather_packed("xt_scales", U8, x_scale_table, two_l)
+        nc.vector.tensor_copy(w1_dealt[:, P // 2 :], w1_halves[1])
+        w1_q = [quantise("w1_%d" % t, P, w1_woven[:, S * t : S * (t + 1)]) for t in range(TILES)]
+
         xo_words = keep.tile([P, S], U32, align_bytes=64)
         for h in range(2):
-            nc.vector.tensor_copy(xo_words[:, HALF * h : HALF * (h + 1)], x_word_table[:].indirect(offs_l[:, 16 * h : 16 * (h + 1)]))
-        y_banks = []
+            nc.vector.tensor_copy(xo_words[:, HALVES[h]], x_word_table[:].indirect(offs_l[:, LIST_HALVES[h]]))
+        y_banks = [bank(t, "y_bank") for t in range(TILES)]
         for t in range(TILES):
-            y_bank = psum.tile([P, S], F32, name="y_bank", tag="bank%d" % (0,1,2,3)[t])
-            for c in (slice(0, HALF), slice(HALF, S)) if t == 0 else (slice(0, S),):
-                product(y_bank[:, c], w1_q[t], block(0), (xo_words[:, c], xo_scales[:, c]))
-            y_banks.append(y_bank)
-        xt_words = gather("xt_words", U32, x_word_table, two_l)
-        d_scale_plane = keep.tile([P, S], U8, tag="w1_codes1", align_bytes=64)
-        nc.vector.memset(d_scale_plane[:].bitcast(I32), 0)
+            for cols in HALVES if t == 0 else (slice(0, S),):
+                product(y_banks[t][:, cols], w1_q[t], block(0), (xo_words, xo_scales), cols)
+
+        xt_words = gather_packed("xt_words", U32, x_word_table, two_l)
+        dk_scale_rows = keep.tile([P, S], U8, tag="w1_1_codes", align_bytes=64)
+        nc.vector.memset(dk_scale_rows[:].bitcast(I32), 0)
         for r in range(4):
-            queue = nc.scalar if r < 4 else nc.sync
-            queue.dma_start(d_scale_plane[r:P:32, :].bitcast(I32), dk_scales[8 * r : P : 32, :].bitcast(I32))
+            nc.scalar.dma_start(dk_scale_rows[r:P:32, :].bitcast(I32), dk_scales[8 * r : P : 32, :].bitcast(I32))
         n4_l = load_list("n4_l", n4)
         n3_l = load_list("n3_l", n3)
-        dk_words = gather("dk_words", U32, d_word_table, k1_l)
+        dk_words = gather_packed("dk_words", U32, d_word_table, k1_l)
 
         w2_codes = keep.tile([P, S], U32, align_bytes=64)
         w2_scales = keep.tile([P, S], U8, align_bytes=64)
 
         def quantise_w2(h, tag):
             woven = keep.tile([P, PACK * HALF], BF16, name="w2_woven%d" % h, tag=tag, align_bytes=64)
-            nc.vector.tensor_copy(
-                woven[:].rearrange("p (c i j) -> p c j i", i=4, j=PACK), w2_raw[h][:].rearrange("p j (c i) -> p c j i", i=4)
+            weave(woven[:], w2_raw[h][:])
+            nc.vector.quantize_mx(
+                out=w2_codes[:, HALVES[h]].bitcast(FP8X4), scales=w2_scales[:, HALVES[h]], in_=woven[:]
             )
-            cols = slice(HALF * h, HALF * (h + 1))
-            nc.vector.quantize_mx(out=w2_codes[:, cols].bitcast(FP8X4), scales=w2_scales[:, cols], in_=woven[:])
 
         quantise_w2(0, "")
-        w2_q = (w2_codes, w2_scales)
 
-        ys = []
+        ds = []
         for t in range(TILES):
             y = keep.tile([P, S], F32, name="y%d" % t)
             nc.scalar.copy(y[:], y_banks[t][:])
@@ -171,108 +182,85 @@ def tile_picked_cdjoinpullbfold_none_p_kernel(
             pa = keep.tile([P, HALF], F32, name="pa%d" % t, align_bytes=64)
             nc.scalar.activation(pa[:], y[:].indirect(n1_l[:]), ACT.Copy)
             nc.vector.tensor_tensor(y[:].indirect(n2_l[:]), pa[:], gate[:], ALU.mult)
-            ys.append(y)
-        z_rows = keep.tile([P, PACK, S], BF16, tag="pa3", align_bytes=64)
-        for t in range(TILES):
-            nc.vector.tensor_scalar(z_rows[:, t, :], ys[t][:], gain[:, t : t + 1], None, ALU.mult)
-        z_wovens = []
+            ds.append(y)
+
+        z_rows = keep.tile([P, PACK, S], BF16, tag="pa%d" % (TILES - 1), align_bytes=64)
+        for cols in HALVES:
+            for t in range(TILES):
+                nc.vector.tensor_scalar(z_rows[:, t, cols], ds[t][:, cols], gain[:, t : t + 1], None, ALU.mult)
+        z_woven = []
         for h in range(2):
             woven = keep.tile([P, PACK * HALF], BF16, name="z_woven%d" % h, align_bytes=64)
-            nc.vector.tensor_copy(
-                woven[:].rearrange("p (c i j) -> p c j i", i=4, j=PACK),
-                z_rows[:, :, HALF * h : HALF * (h + 1)].rearrange("p j (c i) -> p c j i", i=4),
-            )
-            z_wovens.append(woven)
-        z_q = []
-        for h in range(2):
-            codes = keep.tile([P, HALF], U32, name="z_codes%d" % h, align_bytes=64)
-            scales = keep.tile([P, HALF], U8, name="z_scales%d" % h, align_bytes=64)
-            nc.vector.quantize_mx(out=codes[:].bitcast(FP8X4), scales=scales[:], in_=z_wovens[h][:])
-            z_q.append((codes, scales))
+            weave(woven[:], z_rows[:, :, HALVES[h]])
+            z_woven.append(woven)
+        z_q = [quantise("z%d" % h, HALF, z_woven[h][:]) for h in range(2)]
+        quantise_w2(1, "pa%d" % (TILES - 1))
 
-        quantise_w2(1, "pa3")
-        b_banks = []
+        b_banks = [bank(TILES + t, "b_bank") for t in range(TILES)]
         for t in range(TILES):
-            b_bank = psum.tile([P, S], F32, name="b_bank", tag="bank%d" % (4 + t))
-            product(b_bank, (dk_words, d_scale_plane), block(t), (xt_words, xt_scales))
-            b_banks.append(b_bank)
+            product(b_banks[t][:], (dk_words, dk_scale_rows), block(t), (xt_words, xt_scales), slice(0, S))
 
-        opened = {}
+        b_rows, gap_banks, blends_turned, blend_banks, a_banks, a_rows = {}, {}, {}, {}, {}, {}
 
-        def blend_open(t):
-            b = keep.tile([P, S], F32, name="b%d" % t)
-            nc.scalar.activation(b[:], b_banks[t][:], ACT.Copy, scale=0.0625)
-            d_bank = psum.tile([P, S], F32, name="d_bank", tag="bank%d" % t)
-            for jb in range(TILES):
-                nc.tensor.matmul(d_bank[:, block(jb)], b[:, block(jb)], ident[:], start=(jb == 0), stop=False, is_transpose=True)
-            opened[t] = (b, d_bank)
+        def open_gap(t):
+            b_rows[t] = keep.tile([P, S + SPARE], F32, name="b%d" % t)
+            nc.gpsimd.memset(b_rows[t][:, S:], 0.0)
+            nc.scalar.activation(b_rows[t][:, :S], b_banks[t][:], ACT.Copy, scale=0.0625)
+            gap_banks[t] = bank(t, "gap_bank")
+            add_turned(gap_banks[t], b_rows[t], True)
 
-        def blend_close(t):
-            b, d_bank = opened[t]
-            b4 = keep.tile([P, S], F32, name="b4_%d" % t)
-            pull_negated(scalar_negate, "b4", b, n4_l, b4)
-            for jb in range(TILES):
-                nc.tensor.matmul(d_bank[:, block(jb)], b4[:, block(jb)], ident[:], start=False, stop=(jb == TILES - 1), is_transpose=True)
-            blend = keep.tile([P, S], F32, name="blend%d" % t)
-            nc.scalar.activation(blend[:], d_bank[:], ACT.Sigmoid, scale=-1.0)
-            return blend
+        def close_gap(t):
+            minus_b_n4 = keep.tile([P, S], F32, name="minus_b_n4_%d" % t)
+            nc.scalar.activation(minus_b_n4[:], b_rows[t][:].indirect(n4_l[:]), ACT.Copy, scale=-1.0)
+            add_turned(gap_banks[t], minus_b_n4, False)
+            blends_turned[t] = keep.tile([P, S], F32, name="blend%d" % t)
+            nc.scalar.activation(blends_turned[t][:], gap_banks[t][:], ACT.Sigmoid, scale=-1.0)
 
-        def turn_back(t, turned):
-            back_bank = psum.tile([P, S], F32, name="back_bank", tag="bank%d" % t)
-            for jb in range(TILES):
-                nc.tensor.transpose(back_bank[:, block(jb)], turned[:, block(jb)], ident[:])
-            return back_bank
-
-        COPY = "VVSS"
-        blends = []
-        for t in range(2):
-            blend_open(t)
-            blends.append(blend_close(t))
-        blend_open(2)
-        a_banks, rows = {}, {}
+        def turn_blend_back(t):
+            blend_banks[t] = bank(t, "blend_bank")
+            for n in range(TILES):
+                nc.tensor.transpose(blend_banks[t][:, block(n)], blends_turned[t][:, block(n)], ident[:])
 
         def second_product(t):
-            a_banks[t] = psum.tile([P, S], F32, name="a_bank", tag="bank%d" % (4 + t))
+            a_banks[t] = bank(TILES + t, "a_bank")
             for h in range(2):
-                product(a_banks[t][:, HALF * h : HALF * (h + 1)], w2_q, block(t), z_q[h])
+                product(a_banks[t][:, HALVES[h]], (w2_codes, w2_scales), block(t), z_q[h], slice(0, HALF))
 
-        def evacuate(t):
-            rows[t] = keep.tile([P, S], F32, name="a%d" % t)
-            (nc.vector.tensor_copy if COPY[t] == "V" else nc.scalar.copy)(rows[t][:], a_banks[t][:])
+        def evacuate(t, copy):
+            a_rows[t] = keep.tile([P, S], F32, name="a%d" % t)
+            copy(a_rows[t][:], a_banks[t][:])
 
-        def pull_rows(t, engine_copy):
-            a3 = keep.tile([P, S], F32, name="a3_%d" % t)
-            pull_negated(engine_copy, "a3", rows[t], n3_l, a3)
-            return a3
-
-        def scalar_copy(dst, src):
-            nc.scalar.activation(dst, src, ACT.Copy)
-
-        def finish_plain(t, a3, blend_bank, tag, parts=(slice(0, HALF), slice(HALF, S))):
-            a = rows[t]
-            step = keep.tile([P, S], F32, name="step%d" % t, tag=tag)
+        def finish(t, a_n3):
+            a = a_rows[t]
+            step = keep.tile([P, S], F32, name="step%d" % t)
             pull = keep.tile([P, S], F32, name="pull%d" % t)
-            res = keep.tile([P, S], F32, name="res%d" % t)
-            for c in parts:
-                nc.vector.tensor_tensor(step[:, c], a3[:, c], a[:, c], ALU.subtract)
-                nc.vector.tensor_tensor(pull[:, c], blend_bank[:, c], step[:, c], ALU.mult)
-                nc.vector.tensor_tensor(res[:, c], pull[:, c], a[:, c], ALU.add)
-                nc.sync.dma_start(out[block(t), c], res[:, c])
+            result = keep.tile([P, S], F32, name="result%d" % t)
+            for cols in HALVES:
+                nc.vector.tensor_tensor(step[:, cols], a_n3[:, cols], a[:, cols], ALU.subtract)
+                nc.vector.tensor_tensor(pull[:, cols], blend_banks[t][:, cols], step[:, cols], ALU.mult)
+                nc.vector.tensor_tensor(result[:, cols], pull[:, cols], a[:, cols], ALU.add)
+                nc.sync.dma_start(out[block(t), cols], result[:, cols])
 
+        for t in range(2):
+            open_gap(t)
+            close_gap(t)
+        open_gap(2)
         second_product(0)
         second_product(1)
-        evacuate(0)
-        evacuate(1)
-        blends.append(blend_close(2))
-        backs = [turn_back(0, blends[0])]
-        blend_open(3)
+        evacuate(0, nc.vector.tensor_copy)
+        evacuate(1, nc.vector.tensor_copy)
+        close_gap(2)
+        turn_blend_back(0)
+        open_gap(3)
         second_product(2)
         second_product(3)
-        backs.append(turn_back(1, blends[1]))
-        blends.append(blend_close(3))
-        finish_plain(0, pull_rows(0, nc.vector.tensor_copy), backs[0], "")
+        turn_blend_back(1)
+        close_gap(3)
+        finish(0, gather_rows("a_n3_0", nc.vector.tensor_copy, a_rows[0], n3_l))
         for t in range(1, TILES):
-            a3 = pull_rows(t, scalar_copy)
+            a_n3 = gather_rows("a_n3_%d" % t, scalar_copy, a_rows[t], n3_l)
             if t + 1 < TILES:
-                evacuate(t + 1)
-            finish_plain(t, a3, backs[t] if t < len(backs) else turn_back(t, blends[t]), "")
+                evacuate(t + 1, nc.scalar.copy)
+            if t not in blend_banks:
+                turn_blend_back(t)
+            finish(t, a_n3)

from contextlib import ExitStack

import concourse.mybir as mybir
from concourse.masks import make_identity

F32 = mybir.dt.float32
BF16 = mybir.dt.bfloat16
U32 = mybir.dt.uint32
I32 = mybir.dt.int32
U16 = mybir.dt.uint16
U8 = mybir.dt.uint8
FP8X4 = mybir.dt.float8_e4m3fn_x4
ACT = mybir.ActivationFunctionType
ALU = mybir.AluOpType

P = 128
PACK = 4
TABLE = 2048
S = 512
HALF = S // 2
TILES = S // P
HALVES = (slice(0, HALF), slice(HALF, S))
LIST_HALVES = (slice(0, HALF // 16), slice(HALF // 16, S // 16))
SPARE = 8
RUN = 4

FLOPS = 3 * 2 * S * S * S


def tile_picked_cdjoinpullbfold_none_p_kernel(
    tc, x_words, x_scales, w1, gn, w2, d_words, d_scales, offs, n1, n2, two, k1, n3, n4, out
):
    nc = tc.nc
    with ExitStack() as ctx:
        keep = ctx.enter_context(tc.tile_pool(name="keep", bufs=1))
        psum = ctx.enter_context(tc.psum_pool(name="psum", bufs=1))

        def block(n):
            return slice(P * n, P * (n + 1))

        def bank(n, name):
            return psum.tile([P, S], F32, name=name, tag="bank%d" % n)

        def load_list(name, source):
            offsets = keep.tile(list(source.shape), U16, name=name)
            nc.sync.dma_start(offsets[:], source)
            return offsets

        def load_words(name, table):
            words = keep.tile([P, TABLE], U32, name=name)
            nc.sync.dma_start(words[:].bitcast(I32), table[0].rearrange("p n t -> p (n t)").bitcast(I32))
            return words

        def load_weight_half(name, weight, h):
            half = keep.tile([P, PACK, HALF], F32, name="%s_raw%d" % (name, h))
            nc.sync.dma_start(half[:], weight.rearrange("(p j) c -> p j c", j=PACK)[:, :, HALVES[h]])
            return half

        def gather_packed(name, dtype, table, offsets):
            picked = keep.tile([P, S], dtype, name=name, align_bytes=64)
            nc.vector.tensor_copy(picked[:], table[:].indirect(offsets[:]))
            return picked

        def gather_rows(name, copy, rows, offsets):
            picked = keep.tile([P, S], F32, name=name)
            for h in range(2):
                copy(picked[:, HALVES[h]], rows[:].indirect(offsets[:, LIST_HALVES[h]]))
            return picked

        def scalar_copy(dst, src):
            nc.scalar.activation(dst, src, ACT.Copy)

        def weave(woven, rows):
            nc.vector.tensor_copy(
                woven.rearrange("p (c i j) -> p c j i", i=RUN, j=PACK), rows.rearrange("p j (c i) -> p c j i", i=RUN)
            )

        def quantise(name, width, values):
            codes = keep.tile([P, width], U32, name=name + "_codes", align_bytes=64)
            scales = keep.tile([P, width], U8, name=name + "_scales", align_bytes=64)
            nc.vector.quantize_mx(out=codes[:].bitcast(FP8X4), scales=scales[:], in_=values)
            return codes, scales

        def product(result, left, left_cols, right, right_cols):
            nc.tensor.matmul_mx(
                out=result,
                lhsT=left[0][:, left_cols].bitcast(FP8X4),
                lhsT_scale=left[1][:, left_cols],
                rhs=right[0][:, right_cols].bitcast(FP8X4),
                rhs_scale=right[1][:, right_cols],
                start=True,
                stop=True,
            )

        def add_turned(target, rows, opens):
            for n in range(TILES):
                nc.tensor.matmul(
                    target[:, block(n)],
                    rows[:, block(n)],
                    ident[:],
                    start=opens and n == 0,
                    stop=not opens and n == TILES - 1,
                    is_transpose=True,
                )

        x_scale_table = keep.tile([P, TABLE], U8)
        d_scale_table = keep.tile([P, TABLE], U8)
        nc.gpsimd.memset(d_scale_table[:].bitcast(I32), 0)
        nc.vector.memset(x_scale_table[:].bitcast(I32), 0)

        warm = keep.tile([P, 1], F32)
        nc.vector.memset(warm[:], 0.0)
        warmed = keep.tile([P, 1], F32)
        nc.scalar.activation(warmed[:], warm[:], ACT.Sigmoid)

        offs_l = load_list("offs_l", offs)
        k1_l = load_list("k1_l", k1)
        nc.sync.dma_start(d_scale_table[0:P:8, :].bitcast(I32), d_scales[0].bitcast(I32))
        for q in range(4):
            nc.sync.dma_start(
                x_scale_table[32 * q : 32 * q + 4, :].bitcast(I32), x_scales[0, 4 * q : 4 * q + 4, :].bitcast(I32)
            )
        w1_raw = [load_weight_half("w1", w1, 0)]
        two_l = load_list("two_l", two)
        w1_raw.append(load_weight_half("w1", w1, 1))
        x_word_table = load_words("x_word_table", x_words)
        n2_l = load_list("n2_l", n2)
        n1_l = load_list("n1_l", n1)
        w2_raw = [load_weight_half("w2", w2, 0)]
        d_word_table = load_words("d_word_table", d_words)
        w2_raw.append(load_weight_half("w2", w2, 1))
        ident = keep.tile([P, P], F32)
        make_identity(nc, ident[:])
        gain = keep.tile([P, PACK], F32)
        nc.sync.dma_start(gain[:], gn.rearrange("(p t) o -> p (t o)", t=PACK))

        w1_woven = keep.tile([P, PACK * S], BF16, align_bytes=64)
        w1_dealt = w1_woven[:].rearrange("p (t m j) -> p m j t", t=PACK, j=PACK)
        w1_halves = [raw[:].rearrange("p j (m t) -> p m j t", t=PACK) for raw in w1_raw]
        nc.scalar.copy(w1_dealt[:, : P // 2], w1_halves[0])
        dk_scales = gather_packed("dk_scales", U8, d_scale_table, k1_l)
        xo_scales = gather_packed("xo_scales", U8, x_scale_table, offs_l)
        xt_scales = gather_packed("xt_scales", U8, x_scale_table, two_l)
        nc.vector.tensor_copy(w1_dealt[:, P // 2 :], w1_halves[1])
        w1_q = [quantise("w1_%d" % t, P, w1_woven[:, S * t : S * (t + 1)]) for t in range(TILES)]

        xo_words = keep.tile([P, S], U32, align_bytes=64)
        for h in range(2):
            nc.vector.tensor_copy(xo_words[:, HALVES[h]], x_word_table[:].indirect(offs_l[:, LIST_HALVES[h]]))
        y_banks = [bank(t, "y_bank") for t in range(TILES)]
        for t in range(TILES):
            for cols in HALVES if t == 0 else (slice(0, S),):
                product(y_banks[t][:, cols], w1_q[t], block(0), (xo_words, xo_scales), cols)

        xt_words = gather_packed("xt_words", U32, x_word_table, two_l)
        dk_scale_rows = keep.tile([P, S], U8, tag="w1_1_codes", align_bytes=64)
        nc.vector.memset(dk_scale_rows[:].bitcast(I32), 0)
        for r in range(4):
            nc.scalar.dma_start(dk_scale_rows[r:P:32, :].bitcast(I32), dk_scales[8 * r : P : 32, :].bitcast(I32))
        n4_l = load_list("n4_l", n4)
        n3_l = load_list("n3_l", n3)
        dk_words = gather_packed("dk_words", U32, d_word_table, k1_l)

        w2_codes = keep.tile([P, S], U32, align_bytes=64)
        w2_scales = keep.tile([P, S], U8, align_bytes=64)

        def quantise_w2(h, tag):
            woven = keep.tile([P, PACK * HALF], BF16, name="w2_woven%d" % h, tag=tag, align_bytes=64)
            weave(woven[:], w2_raw[h][:])
            nc.vector.quantize_mx(
                out=w2_codes[:, HALVES[h]].bitcast(FP8X4), scales=w2_scales[:, HALVES[h]], in_=woven[:]
            )

        quantise_w2(0, "")

        ds = []
        for t in range(TILES):
            y = keep.tile([P, S], F32, name="y%d" % t)
            nc.scalar.copy(y[:], y_banks[t][:])
            gate = keep.tile([P, HALF], F32, name="gate%d" % t)
            nc.scalar.activation(gate[:], y[:].indirect(n2_l[:]), ACT.Sigmoid)
            pa = keep.tile([P, HALF], F32, name="pa%d" % t, align_bytes=64)
            nc.scalar.activation(pa[:], y[:].indirect(n1_l[:]), ACT.Copy)
            nc.vector.tensor_tensor(y[:].indirect(n2_l[:]), pa[:], gate[:], ALU.mult)
            ds.append(y)

        z_rows = keep.tile([P, PACK, S], BF16, tag="pa%d" % (TILES - 1), align_bytes=64)
        for cols in HALVES:
            for t in range(TILES):
                nc.vector.tensor_scalar(z_rows[:, t, cols], ds[t][:, cols], gain[:, t : t + 1], None, ALU.mult)
        z_woven = []
        for h in range(2):
            woven = keep.tile([P, PACK * HALF], BF16, name="z_woven%d" % h, align_bytes=64)
            weave(woven[:], z_rows[:, :, HALVES[h]])
            z_woven.append(woven)
        z_q = [quantise("z%d" % h, HALF, z_woven[h][:]) for h in range(2)]
        quantise_w2(1, "pa%d" % (TILES - 1))

        b_banks = [bank(TILES + t, "b_bank") for t in range(TILES)]
        for t in range(TILES):
            product(b_banks[t][:], (dk_words, dk_scale_rows), block(t), (xt_words, xt_scales), slice(0, S))

        b_rows, gap_banks, blends_turned, blend_banks, a_banks, a_rows = {}, {}, {}, {}, {}, {}

        def open_gap(t):
            b_rows[t] = keep.tile([P, S + SPARE], F32, name="b%d" % t)
            nc.gpsimd.memset(b_rows[t][:, S:], 0.0)
            nc.scalar.activation(b_rows[t][:, :S], b_banks[t][:], ACT.Copy, scale=0.0625)
            gap_banks[t] = bank(t, "gap_bank")
            add_turned(gap_banks[t], b_rows[t], True)

        def close_gap(t):
            minus_b_n4 = keep.tile([P, S], F32, name="minus_b_n4_%d" % t)
            nc.scalar.activation(minus_b_n4[:], b_rows[t][:].indirect(n4_l[:]), ACT.Copy, scale=-1.0)
            add_turned(gap_banks[t], minus_b_n4, False)
            blends_turned[t] = keep.tile([P, S], F32, name="blend%d" % t)
            nc.scalar.activation(blends_turned[t][:], gap_banks[t][:], ACT.Sigmoid, scale=-1.0)

        def turn_blend_back(t):
            blend_banks[t] = bank(t, "blend_bank")
            for n in range(TILES):
                nc.tensor.transpose(blend_banks[t][:, block(n)], blends_turned[t][:, block(n)], ident[:])

        def second_product(t):
            a_banks[t] = bank(TILES + t, "a_bank")
            for h in range(2):
                product(a_banks[t][:, HALVES[h]], (w2_codes, w2_scales), block(t), z_q[h], slice(0, HALF))

        def evacuate(t, copy):
            a_rows[t] = keep.tile([P, S], F32, name="a%d" % t)
            copy(a_rows[t][:], a_banks[t][:])

        def finish(t, a_n3):
            a = a_rows[t]
            step = keep.tile([P, S], F32, name="step%d" % t)
            pull = keep.tile([P, S], F32, name="pull%d" % t)
            result = keep.tile([P, S], F32, name="result%d" % t)
            for cols in HALVES:
                nc.vector.tensor_tensor(step[:, cols], a_n3[:, cols], a[:, cols], ALU.subtract)
                nc.vector.tensor_tensor(pull[:, cols], blend_banks[t][:, cols], step[:, cols], ALU.mult)
                nc.vector.tensor_tensor(result[:, cols], pull[:, cols], a[:, cols], ALU.add)
                nc.sync.dma_start(out[block(t), cols], result[:, cols])

        for t in range(2):
            open_gap(t)
            close_gap(t)
        open_gap(2)
        second_product(0)
        second_product(1)
        evacuate(0, nc.vector.tensor_copy)
        evacuate(1, nc.vector.tensor_copy)
        close_gap(2)
        turn_blend_back(0)
        open_gap(3)
        second_product(2)
        second_product(3)
        turn_blend_back(1)
        close_gap(3)
        finish(0, gather_rows("a_n3_0", nc.vector.tensor_copy, a_rows[0], n3_l))
        for t in range(1, TILES):
            a_n3 = gather_rows("a_n3_%d" % t, scalar_copy, a_rows[t], n3_l)
            if t + 1 < TILES:
                evacuate(t + 1, nc.scalar.copy)
            if t not in blend_banks:
                turn_blend_back(t)
            finish(t, a_n3)
